import numpy as np, ml_dtypes
CORES = [0,1,16,17,32,33,48,49,64,65,80,81,96,97,112,113]
N = 16
TK = 512
def setup_inputs(rng):
    return {"x": rng.standard_normal((N, 128, TK), dtype=np.float32).astype(ml_dtypes.bfloat16), "w": rng.standard_normal((N, 128, N * 128), dtype=np.float32).astype(ml_dtypes.bfloat16)}
def reference(x, w):
    X, W = x.astype(np.float64), w.astype(np.float64)
    y = np.zeros((N, 128, TK))
    for r in range(N):
        for j in range(N):
            y[r] += W[r][:, 128 * j:128 * j + 128].T @ X[j]
    return {"y": y.astype(ml_dtypes.bfloat16 if x.dtype != np.float64 else np.float64)}

from concourse.bass import DstId, RemoteDMATransfer

NCH = 8
TK = 512
NSLOT = 4

SCRATCH = {
    "ld": ("dram", [NSLOT, 128, TK], "bfloat16"),
    "xs": ("sbuf", [128, 16 * TK], "bfloat16"),
    "ws": ("sbuf", [128, 16 * 128], "bfloat16"),
    "ys": ("sbuf", [128, TK], "bfloat16"),
    "acc": ("psum", [128, TK], "float32"),
}
SEMAPHORES = ["ar%d" % j for j in range(16)] + ["ldx", "lxs", "wa", "wb", "sent", "mm", "cp", "st", "ls"]

SEND = {
    0: [(6, [("M", 3, 2), ("M", 7, 3)]),
        (2, [("P", 1, 0), ("P", 4, 0), ("P", 6, 0)]),
        (4, [("P", 2, 0), ("P", 5, 0)])],
    1: [(7, [("M", 3, 6), ("M", 7, 7)]),
        (5, [("P", 1, 1), ("P", 4, 1), ("P", 6, 1)]),
        (3, [("P", 2, 1), ("P", 5, 1)])],
}
STEP = 2.6
HOP = 2.0

_CACHE = {}


def _even(ci, k):
    return 16 * ci + k


def _odd(ci, k):
    return 16 * ci + 8 + k


def _plan():
    if "p" in _CACHE:
        return _CACHE["p"]
    nodes = {}

    def node(c):
        if c not in nodes:
            nodes[c] = {"val": {}, "t": {}, "slot": {}, "ops": [], "fwd": []}
        return nodes[c]

    def lands(c, j, val, t, in_dram):
        n = node(c)
        n["val"][j] = val
        n["t"][j] = t
        if in_dram:
            n["slot"][j] = len(n["slot"])

    for ci in range(NCH):
        for s in (0, 1):
            j = 2 * ci + s
            me, other = _even(ci, s), _even(ci, 1 - s)
            node(me)["slot"][j] = 0
            node(me)["ops"].append((-9.0, [(j, 0xFFFF, [_even(ci, k) for k, _ in SEND[s]] + [other])]))
            lands(other, j, 16, -1.0, False)
            for k, flow in SEND[s]:
                lands(_even(ci, k), j, 16, -5.0, True)
                dsts = []
                for p, (kind, d, land) in enumerate(flow):
                    cj = (ci + d) % NCH
                    t = STEP * (p + 1)
                    r = [_even(cj, s), _even(cj, 1 - s)]
                    if kind == "M":
                        q = _odd(cj, land)
                        lands(q, j, 8, t, True)
                        node(q)["ops"].append((t, [(j, 0x00FF, r)]))
                        lands(r[0], j, 8, t + HOP + 0.8, False)
                        lands(r[1], j, 8, t + HOP + 2.4, False)
                    elif land < 2:
                        q = _even(cj, land)
                        lands(q, j, 8, t, False)
                        node(q)["fwd"].append((t, j, _even(cj, 1 - land)))
                    else:
                        q = _even(cj, land)
                        lands(q, j, 8, t, True)
                        node(q)["ops"].append((t, [(j, 0xFFFF, r)]))
                        lands(r[0], j, 16, t + HOP, False)
                        lands(r[1], j, 16, t + HOP + 0.8, False)
                    dsts.append(q)
                node(_even(ci, k))["ops"].append((-4.0, [(j, 0x00FF, dsts)]))
    for c in sorted(nodes):
        f = sorted(nodes[c]["fwd"])
        i = 0
        while i < len(f):
            if i + 1 < len(f) and f[i + 1][0] == f[i][0]:
                grp, masks, val = f[i:i + 2], (0x00FF, 0xFF00), 8
            else:
                grp, masks, val = f[i:i + 1], (0xFFFF,), 16
            nodes[c]["ops"].append((grp[0][0], [(j, m, [dst]) for (t, j, dst), m in zip(grp, masks)]))
            for t, j, dst in grp:
                lands(dst, j, val, t + HOP, False)
            i += len(grp)
    for c in nodes:
        nodes[c]["ops"].sort(key=lambda o: o[0])
    _CACHE["p"] = nodes
    return nodes


def _spans(chips):
    out = []
    for c in sorted(chips):
        if out and out[-1][1] == 256 * c:
            out[-1][1] = 256 * (c + 1)
        else:
            out.append([256 * c, 256 * (c + 1)])
    return out


def _bits(m):
    return bin(m).count("1")


def rank_program(g, core, T, topo):
    plan = _plan()
    n = plan.get(core)
    if n is None:
        return
    rank = T.rank_of(core)

    def place(c, j):
        m = plan[c]
        if j in m["slot"]:
            return T.ld[m["slot"][j]]
        return T.xs[:, TK * j:TK * (j + 1)]

    if rank is not None:
        g.sync.dma_start(T.ld[0], T.x[:, :]).then_inc(T.sem.ldx, 16)

    total = 0
    for idx, (t, trs) in enumerate(n["ops"]):
        calls = []
        for j, mask, dsts in trs:
            if j == rank:
                g.wait_ge(T.sem.ldx, 16)
            else:
                g.wait_ge(T.sem["ar%d" % j], n["val"][j])
            ids = []
            for d in dsts:
                rid, pid, _se = topo.addr(d)
                ids.append(DstId(rid=rid, pnc=pid))
            calls.append(RemoteDMATransfer(dst_ids=ids, dma_engine_mask=mask, remote_sem=T.sem["ar%d" % j],
                                           srcs=[place(core, j)], dsts=[place(d, j) for d in dsts], alu_op=0))
            total += _bits(mask)
        g.remote_dma_fused(calls, local_sem=T.sem.ls)
        if rank is not None and idx == 0:
            g.sem_inc(T.sem.sent, 1)
    g.wait_ge(T.sem.ls, total)

    if rank is None:
        return

    ci = rank // 2
    early = _spans([(ci - o) % NCH for o in range(4)])
    late = _spans([(ci - o) % NCH for o in range(4, 8)])
    g.scalar.wait_ge(T.sem.sent, 1)
    for a, b in early:
        g.scalar.dma_start(T.ws[:, a:b], T.w[:, a:b]).then_inc(T.sem.wa, 16)
    g.scalar.dma_start(T.xs[:, TK * rank:TK * (rank + 1)], T.x[:, :]).then_inc(T.sem.lxs, 16)
    g.sync.wait_ge(T.sem.sent, 1)
    for a, b in late:
        g.sync.dma_start(T.ws[:, a:b], T.w[:, a:b]).then_inc(T.sem.wb, 16)

    order = sorted([(n["t"][j], j) for j in n["t"]] + [(3.0, rank)])
    seen = {}
    mm = None
    for i, (t, j) in enumerate(order):
        is_early = (ci - j // 2) % NCH < 4
        if is_early not in seen:
            seen[is_early] = 1
            if is_early:
                g.tensor.wait_ge(T.sem.wa, 16 * len(early))
            else:
                g.tensor.wait_ge(T.sem.wb, 16 * len(late))
        if j == rank:
            g.tensor.wait_ge(T.sem.lxs, 16)
        else:
            g.tensor.wait_ge(T.sem["ar%d" % j], n["val"][j])
        mm = g.tensor.matmul(T.acc[:, :], T.ws[:, 128 * j:128 * (j + 1)], T.xs[:, TK * j:TK * (j + 1)],
                             i == 0, i == len(order) - 1)
    mm.then_inc(T.sem.mm, 1)
    g.vector.wait_ge(T.sem.mm, 1)
    g.vector.tensor_copy(T.ys[:, :], T.acc[:, :]).then_inc(T.sem.cp, 1)
    g.sync.wait_ge(T.sem.cp, 1)
    g.sync.dma_start(T.y[:, :], T.ys[:, :]).then_inc(T.sem.st, 16)
    g.sync.wait_ge(T.sem.st, 16)
